import numpy as np, ml_dtypes
CORES = [16,17,18,19,32,33,34,35]
N = 8
BF = ml_dtypes.bfloat16
def gentries(a):
    return np.ascontiguousarray(a.reshape(8, 16, -1).transpose(0, 2, 1)).reshape(8, -1)
def gtable(e):
    e = np.asarray(e); return np.ascontiguousarray(e.reshape(8, -1, 16).transpose(0, 2, 1)).reshape(128, -1).astype(np.int32)
def f(rng, *shape):
    return (rng.standard_normal(shape, dtype=np.float32) * np.exp2(rng.integers(-2, 3, shape[:-1] + (1,)))).astype(BF)
def wide(rng, *shape):
    v = f(rng, *shape).astype(np.float32); k = shape[:-2] + (1, shape[-1])
    return (v * np.exp2(rng.integers(-6, 7, k)) * (rng.random(k) > 0.0625)).astype(BF)
V, D, C, R = 2048, 4, 48, 2
def ranks(t):
    return t.reshape(8, D, N, V).transpose(2, 0, 1, 3)
def globe(a, bl):
    out = np.zeros((N, 8, D * V), np.int64)
    for r in range(N):
        own = np.broadcast_to(r * V + np.arange(V), (8, V))
        ghosts = (np.arange(N)[:, None, None] * V + bl[:, :, r]).transpose(1, 0, 2).reshape(8, N * C)
        out[r] = np.take_along_axis(np.concatenate([own, ghosts], 1), a[r].reshape(8, D * V).astype(np.int64), 1)
    return out.reshape(N, 8, D, V).transpose(1, 2, 0, 3).reshape(8, D, N * V)
def unpack(nb, bl):
    return np.stack([gentries(t) for t in nb]).reshape(N, 8, D, V), np.stack([gentries(t) for t in bl]).reshape(N, 8, N, C)
def pack(rng, a, bl, v):
    o = np.argsort(rng.random(a.shape), 2); a = np.take_along_axis(a, o, 2); v = np.take_along_axis(v, o, 2)
    return {"nb": np.stack([gtable(t.reshape(8, D * V)) for t in a]), "bl": np.stack([gtable(t.reshape(8, N * C)) for t in bl]),
            "w": np.ascontiguousarray(v).reshape(N, 8, D * V).astype(np.float32).astype(BF), "x": f(rng, N, 128, V)}
def graphs(rng, p):
    bl = np.argsort(rng.random((N, 8, N, V)), axis=-1)[..., :C]
    a = np.full((N, 8, D, V), -1, np.int64)
    for g in range(8):
        for d in range(D):
            for r in range(N):
                for q in range(r):
                    o = rng.permutation(C); u = bl[r, g, q]; t = bl[q, g, r][o]
                    k = (a[r, g, d, u] < 0) & (a[q, g, d, t] < 0) & (rng.random(C) < p)
                    a[r, g, d, u[k]] = V + q * C + o[k]; a[q, g, d, t[k]] = V + r * C + np.flatnonzero(k)
            for r in range(N):
                e = rng.permutation(np.flatnonzero(a[r, g, d] < 0)); h = len(e) // 2
                a[r, g, d, e[:h]] = e[h:2 * h]; a[r, g, d, e[h:2 * h]] = e[:h]
                if len(e) > 2 * h: a[r, g, d, e[-1]] = (e[-1] + 1) % V
        for r in range(N):
            alias = np.full(V, -1, np.int64); alias[bl[r, g, r]] = V + r * C + np.arange(C)
            b = a[r, g]; n = np.where(b < V, alias[np.minimum(b, V - 1)], -1)
            a[r, g] = np.where((n >= 0) & (rng.random((D, V)) < 0.5), n, b)
    return a, bl
def both(a, bl, z):
    return np.array(ranks(np.take_along_axis(z, np.minimum(globe(a, bl), np.arange(N * V)), 2)))
def setup_inputs(rng):
    a, bl = graphs(rng, 0.6)
    return pack(rng, a, bl, both(a, bl, np.exp2(4 * rng.random((8, D, N * V)))))
def setup_inputs_ties(rng):
    a, bl = graphs(rng, 0.6); z = rng.integers(1, 4, (8, D, N * V)).astype(np.float64); z[rng.integers(0, 8)] = 1
    z *= np.exp2(rng.integers(-20, 21, (8, 1, 1)))
    return pack(rng, a, bl, both(a, bl, z))
def setup_inputs_borders(rng):
    a, bl = graphs(rng, 1.0); v = both(a, bl, np.exp2(3 * rng.random((8, D, N * V))))
    far = ranks(globe(a, bl) // V != np.arange(N * V) // V)
    return pack(rng, a, bl, v * np.where(far, 8, 1))
def setup_inputs_hubs(rng):
    a, bl = graphs(rng, 0.6); v = both(a, bl, np.exp2(4 * rng.random((8, D, N * V))))
    for r in range(N):
        for g in range(8):
            e = rng.permutation(V); h = e[:16]; leaves = e[16:V // 2]; b = a[r, g]; c = v[r, g]
            b[:, leaves] = h[rng.integers(0, 16, (D, len(leaves)))]
            b[0, h] = h[np.arange(16) ^ 1]; c[0, h] = 256
    return pack(rng, a, bl, v)
def setup_inputs_any(rng):
    bl = rng.integers(0, V, (N, 8, N, C)); bl[..., C // 2:] = bl[..., :1]; bl[..., 1] = 0; bl[..., 2] = V - 1
    a = rng.integers(0, V + N * C, (N, 8, D, V)); j = np.arange(V)
    a = np.where(ranks(globe(a, bl) == np.arange(N * V)), (j + 1) % V, a)
    o = rng.permutation(8); a[:, o[0]] = (j + 1) % V; a[:, o[1]] = j ^ 1
    for r in range(N):
        for g in o[2:5]:
            q = r ^ 1
            a[r, g, :, bl[r, g, q, 0]] = V + q * C + rng.choice(np.r_[0, C // 2:C], D)
    return pack(rng, a, bl, np.exp2(4 * rng.random((N, 8, D, V))))
def setup_inputs_spread(rng):
    a, bl = graphs(rng, 0.6); z = np.exp2(rng.integers(-3, 4, (8, D, N * V)) + rng.random((8, D, N * V)))
    d = pack(rng, a, bl, both(a, bl, z)); d["x"] = wide(rng, N, 128, V); return d
def check_inputs(d):
    bad = []
    if d["bl"].min() < 0 or d["bl"].max() >= V: bad.append("bl")
    if d["nb"].min() < 0 or d["nb"].max() >= V + N * C: bad.append("nb")
    if not bad and (globe(*unpack(d["nb"], d["bl"])) == np.arange(N * V)).any(): bad.append("own neighbour")
    u = d["w"].astype(np.float32)
    if not (np.isfinite(u).all() and (u > 0).all()): bad.append("w")
    v = np.abs(d["x"].astype(np.float32))
    if not np.isfinite(v).all(): bad.append("x")
    if not 4.0 * D * float(u.max()) * float(v.max()) < 2.0 ** 127: bad.append("range")
    return bad
def reference(nb, bl, w, x):
    i = np.arange(N * V); A = globe(*unpack(nb, bl))
    u = w.astype(np.float64).reshape(N, 8, D, V).transpose(1, 2, 0, 3).reshape(8, D, N * V)
    mate = np.tile(i, (8, 1)); free = np.ones((8, N * V), bool)
    for t in range(R):
        k = np.where(np.take_along_axis(free[:, None], A, 2), u, 0.0)
        P = np.take_along_axis(A, np.argmax(k, 1)[:, None], 1)[:, 0]
        P = np.where(free & (np.max(k, 1) > 0), P, -1)
        hit = (P >= 0) & (np.take_along_axis(P, np.maximum(P, 0), 1) == i)
        mate = np.where(hit, P, mate); free = free & ~hit
    two = mate != i; first = np.minimum(mate, i); rep = first == i
    num = (np.add.accumulate(rep.reshape(8, N, V).astype(np.int64), 2) - 1 + V * np.arange(N)[:, None]).reshape(8, N * V)
    cm = np.take_along_axis(num, first, 1).reshape(8, N, V)
    xx = np.ascontiguousarray(x.astype(np.float64).reshape(N, 8, 16, V).transpose(1, 2, 0, 3)).reshape(8, 16, N * V)
    X = xx + np.where(two[:, None], np.take_along_axis(xx, mate[:, None], 2), 0.0)
    s = np.zeros((8, 16, N * V))
    for d in range(D):
        s += u[:, d, None] * np.take_along_axis(X, A[:, d, None], 2)
    s = s + np.where(two[:, None], np.take_along_axis(s, mate[:, None], 2), 0.0)
    y = np.zeros((8, 16, N * V))
    for g in range(8):
        y[g][:, num[g, rep[g]]] = s[g][:, rep[g]]
    y = np.ascontiguousarray(y.reshape(8, 16, N, V).transpose(2, 0, 1, 3)).reshape(N, 128, V)
    return {"y": y.astype(np.float32), "cm": np.stack([gtable(cm[:, r]) for r in range(N)]).astype(np.float32)}

from concourse.bass import DstId, RemoteDMATransfer
from concourse.mybir import AluOpType as Op, ActivationFunctionType as Fn

N, V, D, C = 8, 2048, 4, 48
NG = N * C
SH = 16
G0 = SH + V
TB = G0 + NG
BIG = 4096
BK = 32768

_F, _B, _I, _H, _U = "float32", "bfloat16", "int32", "float16", "uint16"
_LOG = {n: (w, t) for n, w, t in [
    ("pf", 1, _F), ("pi", 1, _I), ("ci", 1, _I), ("cf", 1, _F), ("c1000", 1, _F), ("p16", 1, _F), ("pX", 1, _F), ("pE", 1, _F),
    ("jj", 144, _F), ("jm", 128, _F), ("v16", 128, _F), ("vB", 128, _F), ("basec", 24, _F), ("cols", 16, _F), ("mc", 16, _F),
    ("idb", 128, _B), ("idf", 128, _F), ("e16", 128, _B), ("ip", 128, _B), ("inn", 128, _B), ("gsh", 144, _H), ("gsf", 144, _F),
    ("hb", 144, _B), ("hh", 144, _H), ("hf", 144, _F), ("gb", 128, _B), ("tri0", 128, _B), ("tri", 128, _B), ("rm", 2048, _H),
    ("zz", 128, _F), ("gid", TB, _F), ("od", 400, _F),
    ("wr", 8192, _B), ("nbi", 512, _I), ("bli", 24, _I), ("xw", TB, _B), ("xo", V, _B), ("wa", 8192, _B),
    ("nbu", 512, _U), ("nbc", 512, _F), ("blu", 24, _U), ("blh", 24, _I), ("blx", 24, _U), ("bll", 24, _I), ("blo", 24, _U),
    ("gidb", NG, _F), ("mask", NG, _F), ("xb", NG, _B),
    ("wT", 384, _F), ("gt", 768, _B), ("code", 512, _F), ("h1", 256, _F), ("q1", 128, _I), ("l1i", 128, _I), ("l1u", 128, _U),
    ("l1s", 128, _F), ("l1f", 128, _F), ("lm", NG, _H), ("l1b", 24, _F), ("l1bu", 24, _U), ("land1", 24, _F), ("d1", 24, _F),
    ("lu1", 24, _U), ("se1", 4, _U), ("ptab1", TB, _F), ("f1b", NG, _B), ("m1b", NG, _B), ("z1b", NG, _B), ("ftab", TB, _B),
    ("m1B", 128, _F), ("l1m", 128, _F), ("cmk", 1536, _F), ("codeb", 96, _F), ("nbbi", 96, _I), ("nbba", 96, _I), ("nbbu", 96, _U),
    ("wb", 1536, _B),
    ("fb", 1536, _B), ("kb", 96, _F), ("h2b", 48, _F), ("q2b", 24, _I), ("l2bi", 24, _I), ("l2b", 24, _F), ("l2bu", 24, _U),
    ("fl", 8192, _B), ("key", 512, _F), ("h2", 256, _F), ("q2", 128, _I), ("l2i", 128, _I), ("l2u", 128, _U), ("l2f", 128, _F),
    ("land2", 24, _F), ("d2", 24, _F), ("lu2", 24, _U), ("se2", 4, _U), ("ptab2", TB, _F),
    ("m2b", NG, _B), ("y2b", NG, _B), ("t2b", NG, _B), ("xmb", NG, _B), ("xm", NG, _B),
    ("pp2", 2048, _H), ("m2B", 128, _F), ("m2l", 128, _F), ("mu", 128, _U),
    ("mg", 2048, _H), ("rep", 128, _B), ("sc", 128, _F), ("nin", 128, _F), ("na", 128, _F), ("nm", 128, _F), ("numh", 128, _H),
    ("numf", 128, _F), ("po", 128, _F), ("posu", 128, _U), ("numt", TB, _F), ("numb", NG, _F), ("cmo", 128, _F),
    ("xt", TB, _F), ("qb", NG, _F), ("sb", NG, _F), ("st", TB, _F),
    ("g2", 2048, _F), ("g3", 2048, _F), ("uu", 2048, _F), ("yw", 4096, _F),
]}
_WHERE, SCRATCH, _fill = {}, {}, {}
for _n, (_w, _t) in _LOG.items():
    if _w <= 512:
        _WHERE[_n] = ("pack_" + _t, _fill.get(_t, 0))
        _fill[_t] = _fill.get(_t, 0) + (_w + 15) // 16 * 16
    else:
        _WHERE[_n] = (_n, 0)
        SCRATCH[_n] = ("sbuf", [128, _w], _t)
for _t, _w in _fill.items():
    SCRATCH["pack_" + _t] = ("sbuf", [128, _w], _t)
_PSUM = {"k%d" % _i: 512 for _i in range(8)}
for _n, _w in _PSUM.items():
    SCRATCH[_n] = ("psum", [128, _w], _F)
    _WHERE[_n] = (_n, 0)
    _LOG[_n] = (_w, _F)
NPOOL = 120
SEMAPHORES = ["e%d" % k for k in range(7)] + ["sent"] + ["s%d" % i for i in range(NPOOL)]


def a(name, c0=0, c1=None, cs=1, p0=0, p1=128, ps=1):
    return (name, c0, _LOG[name][0] if c1 is None else c1, cs, p0, p1, ps)


def ind(win, off):
    return ("ind", win, off)


def _clash(s, t):
    if s[0] != t[0]:
        return False
    if not (s[1] < t[2] and t[1] < s[2] and s[4] < t[5] and t[4] < s[5]):
        return False
    if s[3] == t[3] > 1 and (s[1] - t[1]) % s[3]:
        return False
    if s[6] == t[6] > 1 and (s[4] - t[4]) % s[6]:
        return False
    return True


def _plan(src, topo, cores):
    used, out = set(), {}
    for far in (True, False):
        for dst in cores:
            if dst == src or (topo.chip(dst) != topo.chip(src)) != far:
                continue
            free = [x for x in topo.engines(src, dst) if x not in used]
            e = free[:2] if far else free[-2:]
            used.update(e)
            out[dst] = e
    return out


def rank_program(g, core, T, topo):
    r = T.rank_of(core)
    if r is None:
        return
    ops, acc = [], {}
    mmgroup = {}
    eng = {"v": g.vector, "s": g.scalar, "t": g.tensor, "g": g, "y": g.sync}

    def ap(s):
        if isinstance(s, tuple):
            if s[0] == "ind":
                return ap(s[1]).indirect(ap(s[2]))
            name, b = _WHERE[s[0]]
            cols = slice(b + s[1], b + s[2], s[3]) if s[3] > 1 else slice(b + s[1], b + s[2])
            return T[name][slice(s[4], s[5], s[6]) if s[6] > 1 else slice(s[4], s[5]), cols]
        return s

    def regs(xs):
        out = []
        for s in xs:
            if isinstance(s, tuple):
                out += [s[1], s[2]] if s[0] == "ind" else [s]
        return out

    def op(q, fn, outs, ins, inc=1, stop=None):
        i = len(ops)
        wr, rd = [], regs(ins)
        for o in outs:
            if o[0] == "ind":
                wr.append(o[1])
                rd.append(o[2])
            else:
                wr.append(o)
        dep = set()
        for lst, w in ((rd, False), (wr, True)):
            for s in lst:
                for j, jw, t in acc.get(s[0], ()):
                    if q == "t" and ops[j]["q"] == "t":
                        continue
                    if (s[0] in _PSUM and ops[j]["q"] != q) or ((w or jw) and _clash(s, t)):
                        dep.add(j)
        for lst, w in ((rd, False), (wr, True)):
            for s in lst:
                acc.setdefault(s[0], []).append((i, w, s))
        ops.append({"q": q, "fn": fn, "dep": dep, "inc": inc, "sem": None, "waits": [], "K": 0})
        if q == "t":
            mmgroup.setdefault("open", []).append(i)
            if stop:
                for j in mmgroup["open"]:
                    mmgroup[j] = i
                mmgroup["open"] = []
        return i

    def tt(out, x, y, o):
        op("v", lambda: g.vector.tensor_tensor(out=ap(out), in0=ap(x), in1=ap(y), op=o), [out], [x, y])

    def ts(out, x, s1, o1, s2=None, o2=None):
        if o2 is None:
            op("v", lambda: g.vector.tensor_scalar(out=ap(out), in0=ap(x), scalar1=ap(s1), scalar2=None, op0=o1), [out], [x, s1])
        else:
            op("v", lambda: g.vector.tensor_scalar(out=ap(out), in0=ap(x), scalar1=ap(s1), scalar2=ap(s2), op0=o1, op1=o2),
               [out], [x, s1, s2])

    def tc(out, x):
        op("v", lambda: g.vector.tensor_copy(out=ap(out), in_=ap(x)), [out], [x])

    def ms(out, c):
        op("v", lambda: g.vector.memset(ap(out), c), [out], [])

    def act(out, x, scale=None, bias=None):
        if scale is not None:
            op("s", lambda: g.scalar.activation(out=ap(out), in_=ap(x), func=Fn.Copy, scale=ap(scale)), [out], [x, scale])
        elif bias is not None:
            op("s", lambda: g.scalar.activation(out=ap(out), in_=ap(x), func=Fn.Identity, bias=bias), [out], [x])
        else:
            op("s", lambda: g.scalar.activation(out=ap(out), in_=ap(x), func=Fn.Copy), [out], [x])

    def mm(out, l, rr, start=True, stop=True):
        op("t", lambda: g.tensor.matmul(ap(out), ap(l), ap(rr), start, stop), [out], [l, rr], stop=stop)

    def iota(out, pattern, base, cm):
        if _LOG[out[0]][1] != _I:
            op("g", lambda: g.iota(ap(out), pattern, base, cm, allow_small_or_imprecise_dtypes=True), [out], [])
        else:
            op("g", lambda: g.iota(ap(out), pattern, base, cm), [out], [])

    def dma(q, out, x):
        f = lambda s: ap(s) if isinstance(s, tuple) else s()
        return op(q, lambda: eng[q].dma_start(out=f(out), in_=f(x)), [out] if isinstance(out, tuple) else [], regs([x]), inc=16)

    plan = _plan(core, topo, T.cores)
    expect = sum(len(_plan(c, topo, T.cores)[core]) for c in T.cores if c != core)
    sent = [0]

    def slot(name, q, w, base=0):
        return a(name, base + w * q, base + w * q + w)

    def arrive(k, name, w, base=0):
        i = len(ops)
        for q in range(N):
            if q != r:
                acc.setdefault(name, []).append((i, True, slot(name, q, w, base)))
        ops.append({"q": "r", "fn": None, "dep": set(), "inc": expect, "sem": "e%d" % k, "waits": [], "K": 0})

    def send(k, name, w, dname, base=0):
        dst = slot(dname, r, w, base)

        def fn():
            tr = []
            for q in range(N):
                if q != r:
                    rid, pid, _se = topo.addr(T.cores[q])
                    tr.append(RemoteDMATransfer(dst_ids=[DstId(rid=rid, pnc=pid)], dma_engine_mask=sum(1 << e for e in plan[T.cores[q]]),
                                                remote_sem=T.sem["e%d" % k], src=ap(slot(name, q, w)), dst=ap(dst)))
            g.remote_dma_fused(tr, local_sem=T.sem["sent"])
            sent[0] += sum(len(e) for e in plan.values())
        op("g", fn, [], [slot(name, q, w) for q in range(N) if q != r])

    def fold16(out, lhs, src):
        for c in range(16):
            mm(out, a(lhs, 16 - c, 144 - c), src(c), c == 0, c == 15)

    for k, name, w, base in ((0, "xw", C, G0), (1, "land1", 3, 0), (2, "ftab", C, G0), (3, "land2", 3, 0), (4, "xm", C, 0),
                             (5, "st", C, G0), (6, "numt", C, G0)):
        arrive(k, name, w, base)

    dma("y", a("wr", p1=8), lambda: T.w[:, :])
    dma("s", a("bli"), lambda: T.bl[:, :])
    dma("y", a("nbi"), lambda: T.nb[:, :])
    dma("s", a("xw", SH, G0), lambda: T.x[:, :])
    for c in range(16):
        dma("y", a("wa", 0, 2 * V, p0=c, ps=16), lambda: T.w[:, 0:2 * V])
    dma("y", a("xo"), lambda: T.x[:, :])
    iota(a("pf"), [[1, 1]], 0, 1)
    iota(a("jj"), [[1, 144]], -16, 0)
    iota(a("pi"), [[1, 1]], 0, 1)
    iota(a("cols"), [[1, 16]], 0, 0)
    iota(a("gid", SH, G0), [[1, V]], 0, 0)
    iota(a("jm"), [[16, 8], [0, 16]], 0, 0)
    iota(a("v16"), [[16, 128]], 0, 0)
    iota(a("basec"), [[50, 8], [0, 3]], 1 - (SH + V + C * r - 1024), 0)
    ts(a("idb"), a("jj", 16, 144), a("pf"), Op.is_equal)
    ts(a("ci"), a("pi"), 15, Op.bitwise_and)
    ts(a("ip"), a("jj", 16, 144), a("pf"), Op.is_equal, 4096.0, Op.mult)
    tc(a("cf"), a("ci"))
    ts(a("inn"), a("jj", 16, 144), a("pf"), Op.is_equal, -4096.0, Op.mult)
    tt(a("p16"), a("pf"), a("cf"), Op.subtract)
    ts(a("mc"), a("cols"), a("cf"), Op.is_equal)
    ts(a("gsh"), a("jj"), a("p16"), Op.is_equal)
    ts(a("bll"), a("bli"), 15, Op.bitwise_and)
    ts(a("blh"), a("bli"), 4, Op.logical_shift_right)
    tc(a("blu"), a("bli"))
    tc(a("blo"), a("bll"))
    tc(a("blx"), a("blh"))
    ms(a("xw", 0, SH), 0.0)
    for d in range(D):
        ts(a("nbc", 128 * d, 128 * d + 128), a("nbi", 128 * d, 128 * d + 128), float(SH + (3 - d) * 4096), Op.add)
    for d in range(D):
        for c in range(16):
            mm(a("k%d" % (d // 2), 128 * (d % 2) + c, 128 * (d % 2) + 128, 16),
               a("wr", V * d + c, V * d + V, 16, p1=8), a("idb", 0, 8, p1=8))
    act(a("mask"), ind(a("mc"), a("blo")))
    act(a("wT", 0, 256), a("k0", 0, 256))
    act(a("wT", 256, 384), a("k1", 0, 128))
    act(a("gidb"), ind(a("gid", SH, G0), a("blu")))
    act(a("xb"), ind(a("xw", SH, G0), a("blu")))
    send(0, "xb", C, "xw", G0)

    ms(a("od"), float(BIG))
    ms(a("gid", 0, SH), float(BIG))
    tt(a("gt", 256, 384), a("k0", 128, 256), a("wT", 0, 128), Op.is_gt)
    tt(a("gt", 0, 256), a("k1", 0, 256), a("wT", 0, 256), Op.is_gt)
    tt(a("gt", 512, 640), a("k1", 128, 256), a("wT", 0, 128), Op.is_gt)
    tt(a("gt", 640, 768), a("k1", 0, 128), a("wT", 128, 256), Op.is_gt)
    tt(a("gt", 384, 512), a("k1", 128, 256), a("wT", 256, 384), Op.is_gt)
    g02, g13, g01, g23, g03, g12 = [a("gt", 128 * i, 128 * i + 128) for i in range(6)]
    for d, terms in enumerate((((g01, -1), (g02, -1), (g03, -1)), ((g01, 1), (g13, -1), (g12, -1)),
                               ((g02, 1), (g12, 1), (g23, -1)), ((g13, 1), (g03, 1), (g23, 1)))):
        for i, (s, sg) in enumerate(terms):
            mm(a("k2", 128 * d, 128 * d + 128), s, a("ip" if sg > 0 else "inn"), i == 0, i == 2)
    if r > 0:
        ms(a("gid", G0, G0 + C * r), -1.0)
    if r < 7:
        ms(a("gid", G0 + C * r + C, TB), float(BIG))
    ms(a("ptab1", 0, SH), float(BIG))
    act(slot("gid", r, C, G0), slot("gidb", r, C))
    for q in range(N):
        act(a("od", 50 * q + 1, 50 * q + 49), slot("gidb", q, C))
    act(slot("xw", r, C, G0), slot("xb", r, C))
    tt(a("code"), a("k2"), a("nbc"), Op.add)
    tt(a("h1"), a("code", 0, 256), a("code", 256, 512), Op.max)
    tt(a("q1"), a("h1", 0, 128), a("h1", 128, 256), Op.max)
    ts(a("l1i"), a("q1"), 4095, Op.bitwise_and)
    ts(a("l1s"), a("l1i"), -1024.0, Op.add)
    tc(a("l1u"), a("l1i"))
    tt(a("lm"), ind(a("l1s"), a("blx")), a("mask"), Op.mult)
    fold16(a("k3", 0, 24), "gsh", lambda c: a("lm", c, NG, 16))
    ms(a("ftab", 0, SH), 0.0)
    ts(a("gsf"), a("jj"), a("p16"), Op.is_equal)
    tc(a("l1b"), a("k3", 0, 24))
    send(1, "l1b", 3, "land1")
    dma("y", slot("land1", r, 3), slot("l1b", r, 3))
    ts(a("l1bu"), a("l1b"), 1024.0, Op.add)
    ts(a("se1", 0, 3), slot("l1b", r, 3), 1024.0, Op.add)

    act(a("ptab1", SH, G0), ind(a("gid"), a("l1u")))
    for d in range(D):
        tt(a("cmk", NG * d, NG * d + NG), ind(a("code", 128 * d, 128 * d + 128), a("blx")), a("mask"), Op.mult)
    fold16(a("k3", 0, 96), "gsf", lambda c: a("cmk", c, 1536, 16))
    ts(a("c1000"), a("cf"), 1000.0, Op.mult)
    ts(a("nbu"), a("nbi"), float(SH), Op.add)
    tt(a("pX"), a("c1000"), a("pf"), Op.add)
    ts(a("pE"), a("pf"), 16.0, Op.mult)
    ts(a("hb"), a("jj"), a("pX"), Op.is_equal)
    ts(a("e16"), a("jm"), a("pE"), Op.is_equal)
    ts(a("gb"), a("jm"), a("p16"), Op.is_equal)
    ts(a("tri0"), a("jj", 16, 144), a("pf"), Op.is_lt, -1.0, Op.mult)
    ms(a("zz"), 0.0)
    tt(a("tri"), a("tri0"), a("gb"), Op.mult)
    for d in (0, 1):
        act(a("wb", NG * d, NG * d + NG), ind(a("wa", V * d, V * d + V), a("blu")))
    act(a("yw", V, 2 * V), a("gid", SH, G0), scale=0.0)

    def decode(land, dd, lu, se, ptab):
        c = SH + V + C * r - 1024
        ts(a(dd), a(land), float(c - 1), Op.max, float(c + C), Op.min)
        tt(a(lu), a(dd), a("basec"), Op.add)
        tc(a(ptab, G0, TB), ind(a("od"), a(lu)))
        tc(slot(ptab, r, C, G0), ind(a("gid"), a(se, 0, 3)))

    def wcast(buf, d, c0):
        mm(a(buf), a("e16", p1=8), a("wr", V * d + c0, V * d + c0 + 512, p1=8))

    decode("land1", "d1", "lu1", "se1", "ptab1")
    tt(a("f1b"), ind(a("ptab1"), a("l1bu")), a("gidb"), Op.not_equal)
    send(2, "f1b", C, "ftab", G0)
    act(slot("ftab", r, C, G0), slot("f1b", r, C))
    tt(a("ftab", SH, G0), ind(a("ptab1"), a("l1u")), a("gid", SH, G0), Op.not_equal)
    tc(a("codeb"), a("k3", 0, 96))
    ts(a("m1b"), a("f1b"), -1.0, Op.mult, 1.0, Op.add)
    tc(a("nbbi"), a("codeb"))
    tt(a("z1b"), ind(a("xw"), a("l1bu")), a("m1b"), Op.mult)
    ts(a("nbba"), a("nbbi"), 4095, Op.bitwise_and)
    tc(a("nbbu"), a("nbba"))
    for i in range(8):
        wcast("k%d" % (4 + i % 4), 2 + i // 4, 512 * (i % 4))
        act(a("wa", 2 * V + 512 * i, 2 * V + 512 * i + 512), a("k%d" % (4 + i % 4)))

    act(a("fb", 0, 768), ind(a("ftab"), a("nbbu", 0, 48)))
    tc(a("fb", 768, 1536), ind(a("ftab"), a("nbbu", 48, 96)))
    fold16(a("k1", 0, 96), "hb", lambda c: a("fb", c, 1536, 16))
    for d in (0, 1):
        act(a("fl", V * d, V * d + V), ind(a("ftab"), a("nbu", 128 * d, 128 * d + 128)))
    ms(a("ptab2", 0, SH), float(BIG))
    ts(a("hh"), a("jj"), a("pX"), Op.is_equal)
    ts(a("hf"), a("jj"), a("pX"), Op.is_equal)
    ts(a("idf"), a("jj", 16, 144), a("pf"), Op.is_equal)
    tt(a("kb"), a("codeb"), a("k1", 0, 96), Op.mult)
    tt(a("h2b"), a("kb", 0, 48), a("kb", 48, 96), Op.max)
    tt(a("q2b"), a("h2b", 0, 24), a("h2b", 24, 48), Op.max)
    ts(a("l2bi"), a("q2b"), 4095, Op.bitwise_and)
    ts(a("l2b"), a("l2bi"), -1024.0, Op.add)
    send(3, "l2b", 3, "land2")
    dma("y", slot("land2", r, 3), slot("l2b", r, 3))
    tc(a("l2bu"), a("l2bi"))
    ts(a("se2", 0, 3), slot("l2b", r, 3), 1024.0, Op.add)
    act(a("fl", 2 * V, 2 * V + 768), ind(a("ftab"), a("nbu", 256, 304)))
    tc(a("fl", 2 * V + 768, 3 * V), ind(a("ftab"), a("nbu", 304, 384)))
    tc(a("fl", 3 * V, 4 * V), ind(a("ftab"), a("nbu", 384, 512)))
    for d in range(D):
        fold16(a("k2", 128 * d, 128 * d + 128), "hb", lambda c: a("fl", V * d + c, V * d + V, 16))
    act(a("y2b"), ind(a("xw"), a("l2bu")))
    act(a("k4", 0, NG), a("y2b"))
    act(a("k5", 0, NG), a("z1b"))
    decode("land2", "d2", "lu2", "se2", "ptab2")
    tt(a("key"), a("code"), a("k2"), Op.mult)
    tt(a("h2"), a("key", 0, 256), a("key", 256, 512), Op.max)
    tt(a("q2"), a("h2", 0, 128), a("h2", 128, 256), Op.max)
    ts(a("l2i"), a("q2"), 4095, Op.bitwise_and)
    tc(a("l2u"), a("l2i"))
    act(a("ptab2", SH, SH + 1024), ind(a("gid"), a("l2u", 0, 64)))
    tc(a("ptab2", SH + 1024, G0), ind(a("gid"), a("l2u", 64, 128)))
    tt(a("m2b"), ind(a("ptab2"), a("l2bu")), a("gidb"), Op.is_equal)
    tt(a("t2b"), a("m2b"), a("k4", 0, NG), Op.mult)
    tt(a("xmb"), a("t2b"), a("k5", 0, NG), Op.add)
    send(4, "xmb", C, "xm")
    act(a("pp2", 0, 1024), ind(a("ptab2"), a("l2u", 0, 64)))
    tc(a("pp2", 1024, 2048), ind(a("ptab2"), a("l2u", 64, 128)))
    for d in (2, 3):
        act(a("wb", NG * d, NG * d + NG), ind(a("wa", V * d, V * d + V), a("blu")))
    for c in range(16):
        act(a("rm", 128 * c, 128 * c + 128), a("gb"), scale=a("mc", c, c + 1))
    fold16(a("k3", 0, 128), "hb", lambda c: a("ftab", SH + c, G0, 16))
    fold16(a("k0", 0, 128), "hh", lambda c: a("pp2", c, 2048, 16))
    ts(a("vB"), a("v16"), a("cf"), Op.add)
    ts(a("m1B"), a("k3", 0, 128), -1.0, Op.mult, 1.0, Op.add)
    tc(a("l1f"), a("l1i"))
    tc(a("l2f"), a("l2i"))
    tt(a("l1m"), a("m1B"), a("l1f"), Op.mult)
    tt(a("m2B"), a("k0", 0, 128), a("vB"), Op.is_equal)
    tt(a("m2l"), a("m2B"), a("l2f"), Op.mult)
    tt(a("mu"), a("m2l"), a("l1m"), Op.max)
    tt(a("xt", SH, G0), ind(a("xw"), a("mu")), a("xo"), Op.add)
    act(slot("xm", r, C), slot("xmb", r, C))
    act(a("mg"), ind(a("gid"), a("mu")))
    for d in (2, 3):
        mm(a("k%d" % (4 + d), 0, NG), a("idb"), a("wb", NG * d, NG * d + NG))
    mm(a("k1", 0, NG), a("idb"), a("xw", G0, TB), True, False)
    mm(a("k1", 0, NG), a("idb"), a("xm"), False, True)
    act(a("xt", G0, TB), a("k1", 0, NG))
    wcast("k4", 2, 0)
    wcast("k5", 3, 0)
    fold16(a("k3", 0, 128), "hh", lambda c: a("mg", c, 2048, 16))
    ms(a("xt", 0, SH), 0.0)
    ms(a("st", 0, SH), 0.0)
    act(a("cmk", 0, 768), ind(a("xt"), a("nbbu", 48, 96)))
    tt(a("cmk", 768, 1536), ind(a("xt"), a("nbbu", 0, 48)), a("wb", 0, 768), Op.mult)
    tt(a("k6", 0, NG), a("cmk", 0, NG), a("k6", 0, NG), Op.mult)
    tt(a("qb"), a("cmk", NG, 768), a("k7", 0, NG), Op.mult)
    tt(a("k6", 0, NG), a("cmk", 768, 768 + NG), a("k6", 0, NG), Op.add)
    tt(a("k6", 0, NG), a("qb"), a("k6", 0, NG), Op.add)
    tt(a("sb"), a("cmk", 768 + NG, 1536), a("k6", 0, NG), Op.add)
    send(5, "sb", C, "st", G0)
    wcast("k6", 2, 512)
    wcast("k7", 3, 512)

    def gather23(i):
        for d, b in ((2, "g2"), (3, "g3")):
            act(a(b, 512 * i, 512 * i + 512), ind(a("xt"), a("nbu", 128 * d + 32 * i, 128 * d + 32 * i + 32)))

    def products(i, w2, w3, keep):
        u, ub = 1024 * (i % 2), "ptab2" if i < 2 else "uu"
        for d in (0, 1):
            tt(a(ub, u + 512 * d, u + 512 * d + 512), ind(a("xt"), a("nbu", 128 * d + 32 * i, 128 * d + 32 * i + 32)),
               a("wa", V * d + 512 * i, V * d + 512 * i + 512), Op.mult)
        x2, x3 = a("g2", 512 * i, 512 * i + 512), a("g3", 512 * i, 512 * i + 512)
        tt(a(w2) if keep else x2, x2, a(w2), Op.mult)
        tt(x3, x3, a(w3), Op.mult)

    def sum_v(i, w2):
        u, ub = 1024 * (i % 2), "ptab2" if i < 2 else "uu"
        tt(a(w2), a(ub, u, u + 512), a(w2), Op.add)
        tt(a(w2), a("g3", 512 * i, 512 * i + 512), a(w2), Op.add)
        tt(a("st", SH + 512 * i, SH + 512 * i + 512), a(ub, u + 512, u + 1024), a(w2), Op.add)

    def sum_t(i, k):
        u, ub = 1024 * (i % 2), "ptab2" if i < 2 else "uu"
        xs = (a(ub, u, u + 512), a(ub, u + 512, u + 1024), a("g2", 512 * i, 512 * i + 512), a("g3", 512 * i, 512 * i + 512))
        for j, x in enumerate(xs):
            mm(a(k), a("idf"), x, j == 0, j == 3)

    gather23(0)
    tt(a("rep"), a("k3", 0, 128), a("vB"), Op.is_gt)
    mm(a("k1", 0, 128), a("gb"), a("rep"))
    mm(a("k2", 0, 128), a("tri"), a("rep"))
    op("v", lambda: g.vector.tensor_tensor_scan(ap(a("sc")), ap(a("k1", 0, 128)), ap(a("zz")), 0.0, Op.add, Op.add),
       [a("sc")], [a("k1", 0, 128), a("zz")])
    tt(a("nin"), a("sc"), a("k2", 0, 128), Op.add)
    ts(a("na"), a("nin"), float(BK), Op.add)
    tt(a("nm"), a("na"), a("rep"), Op.mult)
    ts(a("numh"), a("nm"), -float(BK + 1), Op.add)
    products(0, "k4", "k5", False)
    for b in range(4):
        for c in range(16):
            mm(a("k%d" % b, c, 512, 16), a("rm", 128 * c, 128 * c + 128), a("numh", 32 * b, 32 * b + 32))
    wcast("k4", 2, 1024)
    wcast("k5", 3, 1024)
    gather23(1)
    for b in range(4):
        act(a("numt", SH + 512 * b, SH + 512 * b + 512), a("k%d" % b), bias=float(V * r))
    ms(a("numt", 0, SH), -65536.0)
    sum_t(0, "k0")
    act(a("numb"), ind(a("numt", SH, G0), a("blu")))
    act(slot("st", r, C, G0), slot("sb", r, C))
    act(slot("numt", r, C, G0), slot("numb", r, C))
    send(6, "numb", C, "numt", G0)
    products(1, "k6", "k7", False)
    gather23(2)
    sum_t(1, "k1")
    wcast("k6", 2, 1536)
    wcast("k7", 3, 1536)
    gather23(3)
    act(a("st", SH, SH + 512), a("k0"))
    act(a("st", SH + 512, SH + 1024), a("k1"))
    products(2, "k4", "k5", True)
    sum_v(2, "k4")
    ts(a("po"), a("nm"), float(V - 1 - BK), Op.add)
    ts(a("numf"), a("nm"), float(V * r - BK - 1), Op.add)
    tt(a("posu"), a("po"), a("vB"), Op.max)
    products(3, "k6", "k7", True)
    sum_v(3, "k6")
    act(a("ptab1", 0, V), ind(a("numt"), a("mu")))
    fold16(a("k2", 0, 128), "hf", lambda c: a("ptab1", c, V, 16))
    cuts = (128, 96, 48, 16, 0)
    for k1, k0 in zip(cuts, cuts[1:]):
        act(a("g2", 16 * k0, 16 * k1), ind(a("st"), a("mu", k0, k1)))
    last = []
    for i, (k1, k0) in enumerate(zip(cuts, cuts[1:])):
        if i == 3:
            tt(a("cmo"), a("k2", 0, 128), a("numf"), Op.max)
            last.append(dma("y", lambda: T.cm[:, :], a("cmo")))
        tt(ind(a("yw", 0, V + 16 * k1), a("posu", k0, k1)), a("st", SH + 16 * k0, SH + 16 * k1), a("g2", 16 * k0, 16 * k1), Op.add)
        last.append(dma("y", (lambda c0, c1: lambda: T.y[:, c0:c1])(16 * k0, 16 * k1), a("yw", V + 16 * k0, V + 16 * k1)))
    ops.append({"q": "y", "fn": None, "dep": set(last), "inc": 0, "sem": None, "waits": [], "K": 0})

    known = {q: 0 for q in "vstgy"}
    waiters = {}
    for i, o in enumerate(ops):
        if o["q"] == "r":
            continue
        k = known[o["q"]]
        for j in sorted(set(mmgroup.get(j, j) for j in o["dep"]), reverse=True):
            if not k >> j & 1:
                k |= ops[j]["K"] | 1 << j
                o["waits"].append(j)
                waiters.setdefault(j, []).append(i)
        known[o["q"]] = o["K"] = k
    groups = {}
    for j in sorted(waiters):
        if ops[j]["q"] != "r":
            groups.setdefault((ops[j]["q"], tuple(waiters[j])), []).append(j)
    pool, where, need = [], {}, {}
    for (q, ws), js in sorted(groups.items(), key=lambda t: t[1][0]):
        for s, p in enumerate(pool):
            if p[0] == q and all(all(ops[j]["K"] >> w & 1 or (ops[w]["q"] == q and w < j) for w in p[1]) for j in js):
                break
        else:
            s, p = len(pool), [q, (), 0]
            pool.append(p)
        p[1] = ws
        p[2] += sum(ops[j]["inc"] for j in js)
        for j in js:
            where[j], need[j] = "s%d" % s, p[2]
    assert len(pool) <= NPOOL, len(pool)
    for i, o in enumerate(ops):
        if o["q"] == "r":
            continue
        w = {}
        for j in o["waits"]:
            if ops[j]["q"] == "r":
                w[ops[j]["sem"]] = ops[j]["inc"]
            else:
                w[where[j]] = max(w.get(where[j], 0), need[j])
        for s in sorted(w):
            eng[o["q"]].wait_ge(T.sem[s], w[s])
        if o["fn"] is not None:
            x = o["fn"]()
            if i in where:
                x.then_inc(T.sem[where[i]], o["inc"])
    g.wait_ge(T.sem["sent"], sent[0])
